import numpy as np
import ml_dtypes


def mxq(x, axis, fmt="e4m3"):
    dtype, down = {"e4m3": (ml_dtypes.float8_e4m3fn, 7), "e5m2": (ml_dtypes.float8_e5m2, 14)}[fmt]
    v = np.moveaxis(np.asarray(x, np.float32).astype(ml_dtypes.bfloat16).astype(np.float64), axis, -1)
    blocks = v.reshape(v.shape[:-1] + (-1, 32))
    amax = np.abs(blocks).max(-1, keepdims=True)
    byte = np.maximum(np.where(amax > 0, np.frexp(amax)[1] - 1 + 127, 0) - down, 1)
    scale = np.exp2(byte - 127.0)
    codes = (blocks / scale).astype(np.float32).astype(dtype).astype(np.float64)
    return np.moveaxis((codes * scale).reshape(v.shape), -1, axis)


WIDE = False


def mx_kscale(k):
    if not WIDE:
        return np.ones(k)
    levels = np.array([10, -10, 5, -5, 0])
    if k % 512:
        return np.exp2(np.random.permutation(np.resize(levels, k // 32))).repeat(32)
    a = np.empty((k // 512, 16))
    for p in range(k // 512):
        a[p, :8] = np.random.permutation(np.resize(levels, 8))
        for g in range(8):
            far = levels[np.abs(levels - a[p, g]) >= 10]
            a[p, g + 8] = far[np.random.randint(len(far))]
    return np.exp2(a.ravel()).repeat(32)


def f64(x):
    return np.asarray(x).astype(np.float64)


def striped(idx):
    return np.tile(idx.reshape(-1, 16).T, (8, 1)).astype(np.uint16)


def unstriped(offs):
    return offs[:16].T.reshape(-1).astype(np.int64)


E2M1 = np.array([0.0, 0.5, 1.0, 1.5, 2.0, 3.0, 4.0, 6.0, -0.0, -0.5, -1.0, -1.5, -2.0, -3.0, -4.0, -6.0])


def pack_weight(w, fmt):
    k, n = w.shape
    w = f64(np.asarray(w, np.float32).astype(ml_dtypes.bfloat16)).reshape(k // 32, 32, n)
    amax = np.abs(w).max(1)
    if fmt == "e4m3":
        byte = np.frexp(amax)[1] - 1 + 127 - 7
    else:
        mant, ex = np.frexp(amax / 6.0)
        byte = np.where(mant > 0.5, ex, ex - 1) + 127
    byte = np.clip(np.where(amax > 0, byte, 1), 1, 254)
    scaled = (w * np.exp2(127.0 - byte)[:, None, :]).reshape(k, n).astype(np.float32)
    by_word = np.ascontiguousarray(scaled.reshape(k // 512, 128, 4, n).transpose(0, 1, 3, 2))
    if fmt == "e4m3":
        words = by_word.astype(ml_dtypes.float8_e4m3fn).view(np.uint8)
    else:
        c = by_word.astype(ml_dtypes.float4_e2m1fn).view(np.uint8) & 0xF
        words = (c[..., 0::2] | (c[..., 1::2] << 4)).reshape(k // 512, 128, 2 * n)
    return np.ascontiguousarray(words), np.ascontiguousarray(byte.astype(np.uint8).reshape(k // 512, 16, n))


def unpack_weight(words, scales, fmt):
    g, _, n = scales.shape
    words = np.ascontiguousarray(words).reshape(g, 128, n, -1)
    if fmt == "e4m3":
        vals = words.view(ml_dtypes.float8_e4m3fn).astype(np.float64)
    else:
        nib = np.empty((g, 128, n, 4), np.uint8)
        nib[..., 0::2] = words & 0xF
        nib[..., 1::2] = words >> 4
        vals = E2M1[nib]
    vals = vals * np.repeat(np.exp2(scales.astype(np.float64) - 127.0), 8, axis=1)[..., None]
    return vals.transpose(0, 1, 3, 2).reshape(g * 512, n)


K, T, E, C, N = 512, 2048, 12, 256, 128
TOP = 3
PAD = 64


def by_expert(wq, xq):
    return np.concatenate([wq[e].T @ xq[:, e * C:(e + 1) * C] for e in range(E)], axis=1)


def setup_inputs():
    n = np.random.standard_normal
    s = mx_kscale(K)[:, None]
    slot_token = np.empty(E * C, np.int64); pos = np.tile(E * C + np.arange(T) % PAD, (TOP, 1)); taken = np.zeros(T, np.int64)
    liked = np.random.randn(T)
    for e in np.random.permutation(E):
        free = np.flatnonzero(taken < TOP); pick = np.random.permutation(free[np.argsort(-(liked[free] + np.random.gumbel(size=free.size)))[:C]]); slot_token[e * C:(e + 1) * C] = pick
        pos[taken[pick], pick] = e * C + np.arange(C); taken[pick] += 1
    g = np.random.uniform(0.2, 0.8, (TOP, T))
    w = [pack_weight(m, "e2m1") for m in n((E, K, N)) / np.sqrt(K) / s[None]]
    return {
        "xT": (n((K, T)) * s).astype(np.float32),
        "w_words": np.stack([m[0] for m in w]),
        "w_scales": np.stack([m[1] for m in w]),
        "b": (0.3 * n((N, E))).astype(np.float32),
        "gate": np.stack([np.tile(r, (N, 1)) for r in g]).astype(np.float32),
        "offs": striped(slot_token),
        "pos1": striped(pos[0]),
        "pos2": striped(pos[1]),
        "pos3": striped(pos[2]),
    }


def reference(xT, w_words, w_scales, b, gate, offs, pos1, pos2, pos3):
    idx = unstriped(offs)
    w = np.stack([unpack_weight(w_words[e], w_scales[e], "e2m1") for e in range(E)])
    xq = mxq(f64(xT)[:, idx], 0, "e4m3")
    y = by_expert(w, xq)
    y = y + np.repeat(f64(b), C, axis=1)
    y = np.concatenate([y, np.zeros((N, PAD))], axis=1)
    return sum(f64(gate[r]) * y[:, unstriped(p)] for r, p in enumerate((pos1, pos2, pos3)))

@@ -1,0 +1,189 @@
+from contextlib import ExitStack
+
+import concourse.mybir as mybir
+from concourse.masks import make_identity
+
+K, T, E, C, N = 512, 2048, 12, 256, 128
+TOP, PAD = 3, 64
+S = E * C
+FLOPS = 2 * K * N * S
+
+F32 = mybir.dt.float32
+BF16 = mybir.dt.bfloat16
+I32 = mybir.dt.int32
+U32 = mybir.dt.uint32
+U16 = mybir.dt.uint16
+U8 = mybir.dt.uint8
+FP8X4 = mybir.dt.float8_e4m3fn_x4
+FP4X4 = mybir.dt.float4_e2m1fn_x4
+MULT = mybir.AluOpType.mult
+ADD = mybir.AluOpType.add
+IDENT = mybir.ActivationFunctionType.Identity
+COPY = mybir.ActivationFunctionType.Copy
+
+P = 128
+X_CHUNKS = [[512,256],[512,256],[512,256],[256,96],[256,96]]
+SLOT_PIECES = [1024,1024,768,256]
+OUT_CHUNKS = [["T",512],["T",640],["T",640],["V",256]]
+
+
+def tile_moe_ecr_lin_bias_kernel(tc, xT, w_words, w_scales, b, gate, offs, pos1, pos2, pos3, out):
+    nc = tc.nc
+    with ExitStack() as ctx:
+        keep = ctx.enter_context(tc.tile_pool(name="keep", bufs=1))
+        psum = ctx.enter_context(tc.psum_pool(name="psum", bufs=1))
+
+        offs_sb = keep.tile([P, S // 16], U16, name="offs_sb")
+        pos_sb = [keep.tile([P, T // 16], U16, name="pos_sb%d" % r) for r in range(TOP)]
+        codes = keep.tile([P, T], U32, name="codes", align_bytes=64)
+        scales = keep.tile([P, T], U8, name="scales", align_bytes=64)
+        w_sb = keep.tile([P, E * 2 * N], U8, name="w_sb", align_bytes=64)
+        ws_sb = keep.tile([P, E * N], U8, name="ws_sb", align_bytes=64)
+        b_sb = keep.tile([P, E], F32, name="b_sb")
+        y = keep.tile([P, S + PAD], F32, name="y")
+        ident = keep.tile([P, P], F32, name="ident")
+        grow = keep.tile([P, P], F32, name="grow")
+        gcol = keep.tile([P, TOP * 16], F32, name="gcol")
+
+        nc.gpsimd.memset(scales[:].bitcast(I32), 0)
+        nc.gpsimd.memset(ws_sb[:].bitcast(I32), 0)
+        nc.gpsimd.memset(y[:, S:], 0.0)
+        use_t = any(m == "T" for m, w in OUT_CHUNKS)
+        if use_t:
+            nc.gpsimd.memset(grow[:], 0.0)
+        make_identity(nc, ident[:])
+
+        x4 = xT.rearrange("(p j) t -> p j t", j=4)
+        raws = []
+        t0 = 0
+        for i, (w, ws) in enumerate(X_CHUNKS):
+            raw = keep.tile([P, 4, w], F32, name="raw%d" % i)
+            nc.sync.dma_start(out=raw[:], in_=x4[:, :, t0 : t0 + w])
+            raws.append(raw)
+            t0 = t0 + w
+        nc.sync.dma_start(offs_sb[:], offs)
+        nc.sync.dma_start(
+            out=w_sb[:].bitcast(I32).rearrange("p (e c) -> p e c", e=E),
+            in_=w_words.rearrange("e a p c -> p (e a) c").bitcast(I32),
+        )
+        for q in range(4):
+            nc.sync.dma_start(
+                out=ws_sb[q:P:32, :].bitcast(I32).rearrange("p (e c) -> p e c", e=E),
+                in_=w_scales.rearrange("e a (g q) n -> q g (e a) n", q=4)[q].bitcast(I32),
+            )
+        nc.sync.dma_start(out=b_sb[:], in_=b)
+        for r, pos in enumerate((pos1, pos2, pos3)):
+            nc.sync.dma_start(pos_sb[r][:], pos)
+        if use_t:
+            for r in range(TOP):
+                nc.sync.dma_start(out=grow[16 * r : 16 * r + 16, :], in_=gate[r, 0].rearrange("(c t) -> c t", t=P))
+        gates = {}
+        t0 = 0
+        for i, (m, w) in enumerate(OUT_CHUNKS):
+            if m != "T":
+                for r in range(TOP):
+                    g = keep.tile([P, w], F32, name="g%d_%d" % (i, r))
+                    nc.sync.dma_start(out=g[:], in_=gate[r, :, t0 : t0 + w])
+                    gates[(i, r)] = g
+            t0 = t0 + w
+
+        t0 = 0
+        for i, (w, ws) in enumerate(X_CHUNKS):
+            grouped = keep.tile([P, w, 4], BF16, name="grouped%d" % i, align_bytes=64)
+            for eng, a, z in (("s", 0, ws), ("v", ws, w)):
+                if z > a:
+                    dst = grouped[:, a:z, :].rearrange("p (c i) j -> p c j i", i=4)
+                    src = raws[i][:, :, a:z].rearrange("p j (c i) -> p c j i", i=4)
+                    if eng == "s":
+                        nc.scalar.copy(out=dst, in_=src)
+                    else:
+                        nc.vector.tensor_copy(out=dst, in_=src)
+            nc.vector.quantize_mx(
+                out=codes[:, t0 : t0 + w].bitcast(FP8X4),
+                scales=scales[:, t0 : t0 + w],
+                in_=grouped[:].rearrange("p w j -> p (w j)"),
+            )
+            t0 = t0 + w
+
+        if use_t:
+            gps = psum.tile([P, 512], F32, name="gps", tag="back", bufs=2)
+            nc.tensor.transpose(gps[:, :P], grow[:], ident[:])
+            nc.scalar.copy(out=gcol[:], in_=gps[:, : TOP * 16])
+
+        s0 = 0
+        for i, n in enumerate(SLOT_PIECES):
+            gw = keep.tile([P, n], U32, name="gw%d" % i, align_bytes=64)
+            gs = keep.tile([P, n], U8, name="gs%d" % i, align_bytes=64)
+            lst = offs_sb[:, s0 // 16 : (s0 + n) // 16]
+            nc.vector.tensor_copy(gw[:], codes[:].indirect(lst))
+            nc.vector.tensor_copy(gs[:], scales[:].indirect(lst))
+            for c0 in range(0, n, C):
+                e = (s0 + c0) // C
+                acc = psum.tile([P, C], F32, name="acc", tag="acc", bufs=2)
+                nc.tensor.matmul_mx(
+                    out=acc[:],
+                    lhsT=w_sb[:, e * 2 * N : (e + 1) * 2 * N].bitcast(FP4X4),
+                    lhsT_scale=ws_sb[:, e * N : (e + 1) * N],
+                    rhs=gw[:, c0 : c0 + C].bitcast(FP8X4),
+                    rhs_scale=gs[:, c0 : c0 + C],
+                    start=True,
+                    stop=True,
+                )
+                nc.scalar.activation(out=y[:, e * C : (e + 1) * C], in_=acc[:], func=IDENT, bias=b_sb[:, e : e + 1])
+            s0 = s0 + n
+
+        t0 = 0
+        for i, (m, w) in enumerate(OUT_CHUNKS):
+            parts = []
+            for r in range(TOP):
+                part = keep.tile([P, w], F32, name="part%d_%d" % (i, r))
+                picked = y[:].indirect(pos_sb[r][:, t0 // 16 : (t0 + w) // 16])
+                if m == "T":
+                    nc.vector.tensor_copy(part[:], picked)
+                else:
+                    nc.vector.tensor_tensor(part[:], picked, gates[(i, r)][:], MULT)
+                parts.append(part)
+            if m == "V":
+                res = keep.tile([P, w], F32, name="res%d" % i)
+                nc.vector.tensor_tensor(parts[0][:], parts[0][:], parts[1][:], ADD)
+                nc.vector.tensor_tensor(res[:], parts[0][:], parts[2][:], ADD)
+                nc.sync.dma_start(out=out[:, t0 : t0 + w], in_=res[:])
+            else:
+                for g0 in range(0, w, 512):
+                    gwid = min(512, w - g0)
+                    blocks = range(g0, g0 + gwid, P)
+                    turned = []
+                    if m == "T":
+                        for r in range(TOP):
+                            fwd = psum.tile([P, 512], F32, name="fwd", tag="fwd", bufs=4)
+                            for c in blocks:
+                                nc.tensor.transpose(fwd[:, c - g0 : c - g0 + P], parts[r][:, c : c + P], ident[:])
+                            tt = keep.tile([P, gwid], F32, name="tt%d_%d_%d" % (i, g0, r))
+                            for c in blocks:
+                                col = 16 * r + (t0 + c) // P
+                                nc.scalar.activation(
+                                    out=tt[:, c - g0 : c - g0 + P], in_=fwd[:, c - g0 : c - g0 + P], func=COPY, scale=gcol[:, col : col + 1]
+                                )
+                            turned.append(tt)
+                    else:
+                        fwd = psum.tile([P, 512], F32, name="fwd", tag="fwd", bufs=4)
+                        for c in blocks:
+                            for r in range(TOP):
+                                nc.tensor.matmul(
+                                    fwd[:, c - g0 : c - g0 + P], parts[r][:, c : c + P], ident[:],
+                                    start=(r == 0), stop=(r == TOP - 1), is_transpose=True,
+                                )
+                        tt = keep.tile([P, gwid], F32, name="tt%d_%d" % (i, g0))
+                        nc.scalar.copy(out=tt[:], in_=fwd[:, :gwid])
+                        turned.append(tt)
+                    back = psum.tile([P, 512], F32, name="back", tag="back", bufs=2)
+                    for c in blocks:
+                        for r, tt in enumerate(turned):
+                            nc.tensor.matmul(
+                                back[:, c - g0 : c - g0 + P], tt[:, c - g0 : c - g0 + P], ident[:],
+                                start=(r == 0), stop=(r == len(turned) - 1), is_transpose=True,
+                            )
+                    res = keep.tile([P, gwid], F32, name="res%d_%d" % (i, g0))
+                    nc.scalar.copy(out=res[:], in_=back[:, :gwid])
+                    nc.sync.dma_start(out=out[:, t0 + g0 : t0 + g0 + gwid], in_=res[:])
+            t0 = t0 + w

@@ -22,9 +22,9 @@ IDENT = mybir.ActivationFunctionType.Identity
 COPY = mybir.ActivationFunctionType.Copy
 
 P = 128
-X_CHUNKS = [[512,256],[512,256],[512,256],[256,96],[256,96]]
+X_CHUNKS = [[512,256],[512,256],[512,256],[256,128],[128,64],[128,48]]
 SLOT_PIECES = [1024,1024,768,256]
-OUT_CHUNKS = [["T",512],["T",640],["T",640],["V",256]]
+OUT_CHUNKS = [["T",512],["T",640],["T",512],["V",384]]
 
 
 def tile_moe_ecr_lin_bias_kernel(tc, xT, w_words, w_scales, b, gate, offs, pos1, pos2, pos3, out):
@@ -106,7 +106,7 @@ def tile_moe_ecr_lin_bias_kernel(tc, xT, w_words, w_scales, b, gate, offs, pos1,
             t0 = t0 + w
 
         if use_t:
-            gps = psum.tile([P, 512], F32, name="gps", tag="back", bufs=2)
+            gps = psum.tile([P, 512], F32, name="gps", tag="fwd", bufs=4)
             nc.tensor.transpose(gps[:, :P], grow[:], ident[:])
             nc.scalar.copy(out=gcol[:], in_=gps[:, : TOP * 16])
 
@@ -119,7 +119,7 @@ def tile_moe_ecr_lin_bias_kernel(tc, xT, w_words, w_scales, b, gate, offs, pos1,
             nc.vector.tensor_copy(gs[:], scales[:].indirect(lst))
             for c0 in range(0, n, C):
                 e = (s0 + c0) // C
-                acc = psum.tile([P, C], F32, name="acc", tag="acc", bufs=2)
+                acc = psum.tile([P, C], F32, name="acc", tag="acc", bufs=4)
                 nc.tensor.matmul_mx(
                     out=acc[:],
                     lhsT=w_sb[:, e * 2 * N : (e + 1) * 2 * N].bitcast(FP4X4),
@@ -134,56 +134,38 @@ def tile_moe_ecr_lin_bias_kernel(tc, xT, w_words, w_scales, b, gate, offs, pos1,
 
         t0 = 0
         for i, (m, w) in enumerate(OUT_CHUNKS):
-            parts = []
-            for r in range(TOP):
-                part = keep.tile([P, w], F32, name="part%d_%d" % (i, r))
-                picked = y[:].indirect(pos_sb[r][:, t0 // 16 : (t0 + w) // 16])
-                if m == "T":
-                    nc.vector.tensor_copy(part[:], picked)
-                else:
-                    nc.vector.tensor_tensor(part[:], picked, gates[(i, r)][:], MULT)
-                parts.append(part)
             if m == "V":
+                parts = []
+                for r in range(TOP):
+                    part = keep.tile([P, w], F32, name="part%d_%d" % (i, r))
+                    picked = y[:].indirect(pos_sb[r][:, t0 // 16 : (t0 + w) // 16])
+                    nc.vector.tensor_tensor(part[:], picked, gates[(i, r)][:], MULT)
+                    parts.append(part)
                 res = keep.tile([P, w], F32, name="res%d" % i)
                 nc.vector.tensor_tensor(parts[0][:], parts[0][:], parts[1][:], ADD)
                 nc.vector.tensor_tensor(res[:], parts[0][:], parts[2][:], ADD)
                 nc.sync.dma_start(out=out[:, t0 : t0 + w], in_=res[:])
             else:
-                for g0 in range(0, w, 512):
-                    gwid = min(512, w - g0)
-                    blocks = range(g0, g0 + gwid, P)
-                    turned = []
-                    if m == "T":
-                        for r in range(TOP):
-                            fwd = psum.tile([P, 512], F32, name="fwd", tag="fwd", bufs=4)
-                            for c in blocks:
-                                nc.tensor.transpose(fwd[:, c - g0 : c - g0 + P], parts[r][:, c : c + P], ident[:])
-                            tt = keep.tile([P, gwid], F32, name="tt%d_%d_%d" % (i, g0, r))
-                            for c in blocks:
-                                col = 16 * r + (t0 + c) // P
-                                nc.scalar.activation(
-                                    out=tt[:, c - g0 : c - g0 + P], in_=fwd[:, c - g0 : c - g0 + P], func=COPY, scale=gcol[:, col : col + 1]
-                                )
-                            turned.append(tt)
-                    else:
+                groups = [(g0, min(512, w - g0)) for g0 in range(0, w, 512)]
+                backs = [psum.tile([P, 512], F32, name="back", tag="acc", bufs=4) for g in groups]
+                for r in range(TOP):
+                    part = keep.tile([P, w], F32, name="part%d_%d" % (i, r))
+                    nc.vector.tensor_copy(part[:], y[:].indirect(pos_sb[r][:, t0 // 16 : (t0 + w) // 16]))
+                    for (g0, gwid), back in zip(groups, backs):
                         fwd = psum.tile([P, 512], F32, name="fwd", tag="fwd", bufs=4)
-                        for c in blocks:
-                            for r in range(TOP):
-                                nc.tensor.matmul(
-                                    fwd[:, c - g0 : c - g0 + P], parts[r][:, c : c + P], ident[:],
-                                    start=(r == 0), stop=(r == TOP - 1), is_transpose=True,
-                                )
-                        tt = keep.tile([P, gwid], F32, name="tt%d_%d" % (i, g0))
-                        nc.scalar.copy(out=tt[:], in_=fwd[:, :gwid])
-                        turned.append(tt)
-                    back = psum.tile([P, 512], F32, name="back", tag="back", bufs=2)
-                    for c in blocks:
-                        for r, tt in enumerate(turned):
+                        for c in range(0, gwid, P):
+                            nc.tensor.transpose(fwd[:, c : c + P], part[:, g0 + c : g0 + c + P], ident[:])
+                        tt = keep.tile([P, gwid], F32, name="tt%d_%d_%d" % (i, g0, r))
+                        for c in range(0, gwid, P):
+                            col = 16 * r + (t0 + g0 + c) // P
+                            nc.scalar.activation(out=tt[:, c : c + P], in_=fwd[:, c : c + P], func=COPY, scale=gcol[:, col : col + 1])
+                        for c in range(0, gwid, P):
                             nc.tensor.matmul(
-                                back[:, c - g0 : c - g0 + P], tt[:, c - g0 : c - g0 + P], ident[:],
-                                start=(r == 0), stop=(r == len(turned) - 1), is_transpose=True,
+                                back[:, c : c + P], tt[:, c : c + P], ident[:],
+                                start=(r == 0 and c == 0), stop=(r == TOP - 1 and c == gwid - P), is_transpose=True,
                             )
+                for (g0, gwid), back in zip(groups, backs):
                     res = keep.tile([P, gwid], F32, name="res%d_%d" % (i, g0))
                     nc.scalar.copy(out=res[:], in_=back[:, :gwid])
-                    nc.sync.dma_start(out=out[:, t0 + g0 : t0 + g0 + gwid], in_=res[:])
+                    nc.scalar.dma_start(out=out[:, t0 + g0 : t0 + g0 + gwid], in_=res[:])
             t0 = t0 + w

@@ -24,7 +24,7 @@ COPY = mybir.ActivationFunctionType.Copy
 P = 128
 X_CHUNKS = [[512,256],[512,256],[512,256],[256,128],[128,64],[128,48]]
 SLOT_PIECES = [1024,1024,768,256]
-OUT_CHUNKS = [["T",512],["T",640],["T",512],["V",384]]
+OUT_CHUNKS = [["P",512],["P",512],["P",512],["P",256],["V",256]]
 
 
 def tile_moe_ecr_lin_bias_kernel(tc, xT, w_words, w_scales, b, gate, offs, pos1, pos2, pos3, out):
@@ -81,10 +81,9 @@ def tile_moe_ecr_lin_bias_kernel(tc, xT, w_words, w_scales, b, gate, offs, pos1,
         t0 = 0
         for i, (m, w) in enumerate(OUT_CHUNKS):
             if m != "T":
-                for r in range(TOP):
-                    g = keep.tile([P, w], F32, name="g%d_%d" % (i, r))
-                    nc.sync.dma_start(out=g[:], in_=gate[r, :, t0 : t0 + w])
-                    gates[(i, r)] = g
+                g = keep.tile([P, TOP, w], F32, name="g%d" % i)
+                nc.sync.dma_start(out=g[:], in_=gate.rearrange("r n t -> n r t")[:, :, t0 : t0 + w])
+                gates[i] = g
             t0 = t0 + w
 
         t0 = 0
@@ -106,7 +105,7 @@ def tile_moe_ecr_lin_bias_kernel(tc, xT, w_words, w_scales, b, gate, offs, pos1,
             t0 = t0 + w
 
         if use_t:
-            gps = psum.tile([P, 512], F32, name="gps", tag="fwd", bufs=4)
+            gps = psum.tile([P, 512], F32, name="gps", tag="back", bufs=2)
             nc.tensor.transpose(gps[:, :P], grow[:], ident[:])
             nc.scalar.copy(out=gcol[:], in_=gps[:, : TOP * 16])
 
@@ -134,38 +133,31 @@ def tile_moe_ecr_lin_bias_kernel(tc, xT, w_words, w_scales, b, gate, offs, pos1,
 
         t0 = 0
         for i, (m, w) in enumerate(OUT_CHUNKS):
+            parts = []
+            if m == "P":
+                fwd = psum.tile([P, 512], F32, name="fwd", tag="fwd", bufs=2)
+            for r in range(TOP):
+                part = keep.tile([P, w], F32, name="part%d_%d" % (i, r))
+                picked = y[:].indirect(pos_sb[r][:, t0 // 16 : (t0 + w) // 16])
+                nc.vector.tensor_tensor(part[:], picked, gates[i][:, r, :], MULT)
+                parts.append(part)
+                if m == "P":
+                    for c in range(0, w, P):
+                        nc.tensor.matmul(
+                            fwd[:, c : c + P], part[:, c : c + P], ident[:],
+                            start=(r == 0 and c == 0), stop=(r == TOP - 1 and c == w - P), is_transpose=True,
+                        )
+            res = keep.tile([P, w], F32, name="res%d" % i)
             if m == "V":
-                parts = []
-                for r in range(TOP):
-                    part = keep.tile([P, w], F32, name="part%d_%d" % (i, r))
-                    picked = y[:].indirect(pos_sb[r][:, t0 // 16 : (t0 + w) // 16])
-                    nc.vector.tensor_tensor(part[:], picked, gates[(i, r)][:], MULT)
-                    parts.append(part)
-                res = keep.tile([P, w], F32, name="res%d" % i)
                 nc.vector.tensor_tensor(parts[0][:], parts[0][:], parts[1][:], ADD)
                 nc.vector.tensor_tensor(res[:], parts[0][:], parts[2][:], ADD)
                 nc.sync.dma_start(out=out[:, t0 : t0 + w], in_=res[:])
             else:
-                groups = [(g0, min(512, w - g0)) for g0 in range(0, w, 512)]
-                backs = [psum.tile([P, 512], F32, name="back", tag="acc", bufs=4) for g in groups]
-                for r in range(TOP):
-                    part = keep.tile([P, w], F32, name="part%d_%d" % (i, r))
-                    nc.vector.tensor_copy(part[:], y[:].indirect(pos_sb[r][:, t0 // 16 : (t0 + w) // 16]))
-                    for (g0, gwid), back in zip(groups, backs):
-                        fwd = psum.tile([P, 512], F32, name="fwd", tag="fwd", bufs=4)
-                        for c in range(0, gwid, P):
-                            nc.tensor.transpose(fwd[:, c : c + P], part[:, g0 + c : g0 + c + P], ident[:])
-                        tt = keep.tile([P, gwid], F32, name="tt%d_%d_%d" % (i, g0, r))
-                        for c in range(0, gwid, P):
-                            col = 16 * r + (t0 + g0 + c) // P
-                            nc.scalar.activation(out=tt[:, c : c + P], in_=fwd[:, c : c + P], func=COPY, scale=gcol[:, col : col + 1])
-                        for c in range(0, gwid, P):
-                            nc.tensor.matmul(
-                                back[:, c : c + P], tt[:, c : c + P], ident[:],
-                                start=(r == 0 and c == 0), stop=(r == TOP - 1 and c == gwid - P), is_transpose=True,
-                            )
-                for (g0, gwid), back in zip(groups, backs):
-                    res = keep.tile([P, gwid], F32, name="res%d_%d" % (i, g0))
-                    nc.scalar.copy(out=res[:], in_=back[:, :gwid])
-                    nc.scalar.dma_start(out=out[:, t0 + g0 : t0 + g0 + gwid], in_=res[:])
+                tt = keep.tile([P, w], F32, name="tt%d" % i)
+                nc.scalar.copy(out=tt[:], in_=fwd[:, :w])
+                back = psum.tile([P, 512], F32, name="back", tag="back", bufs=2)
+                for c in range(0, w, P):
+                    nc.tensor.transpose(back[:, c : c + P], tt[:, c : c + P], ident[:])
+                nc.scalar.copy(out=res[:], in_=back[:, :w])
+                nc.scalar.dma_start(out=out[:, t0 : t0 + w], in_=res[:])
             t0 = t0 + w

@@ -23,8 +23,8 @@ COPY = mybir.ActivationFunctionType.Copy
 
 P = 128
 X_CHUNKS = [[512,256],[512,256],[512,256],[256,128],[128,64],[128,48]]
-SLOT_PIECES = [1024,1024,768,256]
-OUT_CHUNKS = [["P",512],["P",512],["P",512],["P",256],["V",256]]
+SLOT_PIECES = [1280,1024,512,256]
+OUT_CHUNKS = [["T",512],["P",512],["P",512],["P",256],["V",256]]
 
 
 def tile_moe_ecr_lin_bias_kernel(tc, xT, w_words, w_scales, b, gate, offs, pos1, pos2, pos3, out):
@@ -118,7 +118,7 @@ def tile_moe_ecr_lin_bias_kernel(tc, xT, w_words, w_scales, b, gate, offs, pos1,
             nc.vector.tensor_copy(gs[:], scales[:].indirect(lst))
             for c0 in range(0, n, C):
                 e = (s0 + c0) // C
-                acc = psum.tile([P, C], F32, name="acc", tag="acc", bufs=4)
+                acc = psum.tile([P, C], F32, name="acc", tag="acc", bufs=3)
                 nc.tensor.matmul_mx(
                     out=acc[:],
                     lhsT=w_sb[:, e * 2 * N : (e + 1) * 2 * N].bitcast(FP4X4),
@@ -133,9 +133,31 @@ def tile_moe_ecr_lin_bias_kernel(tc, xT, w_words, w_scales, b, gate, offs, pos1,
 
         t0 = 0
         for i, (m, w) in enumerate(OUT_CHUNKS):
+            if m == "T":
+                back = psum.tile([P, 512], F32, name="back", tag="back", bufs=2)
+                for r in range(TOP):
+                    part = keep.tile([P, w], F32, name="part%d_%d" % (i, r))
+                    nc.vector.tensor_copy(part[:], y[:].indirect(pos_sb[r][:, t0 // 16 : (t0 + w) // 16]))
+                    fwd = psum.tile([P, 512], F32, name="fwd", tag="fwd", bufs=3)
+                    for c in range(0, w, P):
+                        nc.tensor.transpose(fwd[:, c : c + P], part[:, c : c + P], ident[:])
+                    tt = keep.tile([P, w], F32, name="tt%d_%d" % (i, r))
+                    for c in range(0, w, P):
+                        col = 16 * r + (t0 + c) // P
+                        nc.scalar.activation(out=tt[:, c : c + P], in_=fwd[:, c : c + P], func=COPY, scale=gcol[:, col : col + 1])
+                    for c in range(0, w, P):
+                        nc.tensor.matmul(
+                            back[:, c : c + P], tt[:, c : c + P], ident[:],
+                            start=(r == 0 and c == 0), stop=(r == TOP - 1 and c == w - P), is_transpose=True,
+                        )
+                res = keep.tile([P, w], F32, name="res%d" % i)
+                nc.scalar.copy(out=res[:], in_=back[:, :w])
+                nc.scalar.dma_start(out=out[:, t0 : t0 + w], in_=res[:])
+                t0 = t0 + w
+                continue
             parts = []
             if m == "P":
-                fwd = psum.tile([P, 512], F32, name="fwd", tag="fwd", bufs=2)
+                fwd = psum.tile([P, 512], F32, name="fwd", tag="fwd", bufs=3)
             for r in range(TOP):
                 part = keep.tile([P, w], F32, name="part%d_%d" % (i, r))
                 picked = y[:].indirect(pos_sb[r][:, t0 // 16 : (t0 + w) // 16])

@@ -4,7 +4,8 @@ import concourse.mybir as mybir
 from concourse.masks import make_identity
 
 K, T, E, C, N = 512, 2048, 12, 256, 128
-TOP, PAD = 3, 64
+TOP = 3
+PAD = 64
 S = E * C
 FLOPS = 2 * K * N * S
 
@@ -18,13 +19,30 @@ FP8X4 = mybir.dt.float8_e4m3fn_x4
 FP4X4 = mybir.dt.float4_e2m1fn_x4
 MULT = mybir.AluOpType.mult
 ADD = mybir.AluOpType.add
-IDENT = mybir.ActivationFunctionType.Identity
+IDENTITY = mybir.ActivationFunctionType.Identity
 COPY = mybir.ActivationFunctionType.Copy
 
 P = 128
-X_CHUNKS = [[512,256],[512,256],[512,256],[256,128],[128,64],[128,48]]
-SLOT_PIECES = [1280,1024,512,256]
-OUT_CHUNKS = [["T",512],["P",512],["P",512],["P",256],["V",256]]
+PACK = 4
+STRIPE = 16
+BANK = 512
+RUN = 4
+
+X_LOADS = [(512, 256), (512, 256), (512, 256), (256, 128), (128, 64), (128, 48)]
+
+SLOT_PIECES = [1280, 1024, 512, 256]
+
+TURNED_GATE = 512
+PSUM_SUMS = [512, 512, 256]
+VECTOR_SUM = 256
+assert TURNED_GATE + sum(PSUM_SUMS) + VECTOR_SUM == T
+SQUARES = TURNED_GATE // P
+
+PRODUCT_BANKS, TURN_BANKS, BACK_BANKS = 3, 3, 2
+
+
+def entries(list_tile, first, count):
+    return list_tile[:, first // STRIPE : (first + count) // STRIPE]
 
 
 def tile_moe_ecr_lin_bias_kernel(tc, xT, w_words, w_scales, b, gate, offs, pos1, pos2, pos3, out):
@@ -33,153 +51,150 @@ def tile_moe_ecr_lin_bias_kernel(tc, xT, w_words, w_scales, b, gate, offs, pos1,
         keep = ctx.enter_context(tc.tile_pool(name="keep", bufs=1))
         psum = ctx.enter_context(tc.psum_pool(name="psum", bufs=1))
 
-        offs_sb = keep.tile([P, S // 16], U16, name="offs_sb")
-        pos_sb = [keep.tile([P, T // 16], U16, name="pos_sb%d" % r) for r in range(TOP)]
-        codes = keep.tile([P, T], U32, name="codes", align_bytes=64)
-        scales = keep.tile([P, T], U8, name="scales", align_bytes=64)
-        w_sb = keep.tile([P, E * 2 * N], U8, name="w_sb", align_bytes=64)
-        ws_sb = keep.tile([P, E * N], U8, name="ws_sb", align_bytes=64)
-        b_sb = keep.tile([P, E], F32, name="b_sb")
+        offs_sb = keep.tile([P, S // STRIPE], U16, name="offs_sb")
+        pos_sb = [keep.tile([P, T // STRIPE], U16, name="pos_sb%d" % r) for r in range(TOP)]
+        token_words = keep.tile([P, T], U32, name="token_words", align_bytes=64)
+        token_scales = keep.tile([P, T], U8, name="token_scales", align_bytes=64)
+        weight_words = keep.tile([P, E * 2 * N], U8, name="weight_words", align_bytes=64)
+        weight_scales = keep.tile([P, E * N], U8, name="weight_scales", align_bytes=64)
+        bias = keep.tile([P, E], F32, name="bias")
         y = keep.tile([P, S + PAD], F32, name="y")
-        ident = keep.tile([P, P], F32, name="ident")
-        grow = keep.tile([P, P], F32, name="grow")
-        gcol = keep.tile([P, TOP * 16], F32, name="gcol")
+        identity = keep.tile([P, P], F32, name="identity")
+        gate_rows = keep.tile([P, P], F32, name="gate_rows")
+        gate_cols = keep.tile([P, TOP * SQUARES], F32, name="gate_cols")
 
-        nc.gpsimd.memset(scales[:].bitcast(I32), 0)
-        nc.gpsimd.memset(ws_sb[:].bitcast(I32), 0)
+        nc.gpsimd.memset(token_scales[:].bitcast(I32), 0)
+        nc.gpsimd.memset(weight_scales[:].bitcast(I32), 0)
         nc.gpsimd.memset(y[:, S:], 0.0)
-        use_t = any(m == "T" for m, w in OUT_CHUNKS)
-        if use_t:
-            nc.gpsimd.memset(grow[:], 0.0)
-        make_identity(nc, ident[:])
+        nc.gpsimd.memset(gate_rows[:], 0.0)
+        make_identity(nc, identity[:])
 
-        x4 = xT.rearrange("(p j) t -> p j t", j=4)
-        raws = []
+        x_rows = xT.rearrange("(p j) t -> p j t", j=PACK)
+        x_tiles = []
         t0 = 0
-        for i, (w, ws) in enumerate(X_CHUNKS):
-            raw = keep.tile([P, 4, w], F32, name="raw%d" % i)
-            nc.sync.dma_start(out=raw[:], in_=x4[:, :, t0 : t0 + w])
-            raws.append(raw)
-            t0 = t0 + w
+        for i, (tokens, on_scalar) in enumerate(X_LOADS):
+            x_tile = keep.tile([P, PACK, tokens], F32, name="x_tile%d" % i)
+            nc.sync.dma_start(out=x_tile[:], in_=x_rows[:, :, t0 : t0 + tokens])
+            x_tiles.append(x_tile)
+            t0 = t0 + tokens
         nc.sync.dma_start(offs_sb[:], offs)
         nc.sync.dma_start(
-            out=w_sb[:].bitcast(I32).rearrange("p (e c) -> p e c", e=E),
+            out=weight_words[:].bitcast(I32).rearrange("p (e c) -> p e c", e=E),
             in_=w_words.rearrange("e a p c -> p (e a) c").bitcast(I32),
         )
-        for q in range(4):
+        for d in range(4):
             nc.sync.dma_start(
-                out=ws_sb[q:P:32, :].bitcast(I32).rearrange("p (e c) -> p e c", e=E),
-                in_=w_scales.rearrange("e a (g q) n -> q g (e a) n", q=4)[q].bitcast(I32),
+                out=weight_scales[d:P:32, :].bitcast(I32).rearrange("g (e c) -> g e c", e=E),
+                in_=w_scales.rearrange("e a (g d) n -> d g (e a) n", d=4)[d].bitcast(I32),
             )
-        nc.sync.dma_start(out=b_sb[:], in_=b)
+        nc.sync.dma_start(out=bias[:], in_=b)
         for r, pos in enumerate((pos1, pos2, pos3)):
             nc.sync.dma_start(pos_sb[r][:], pos)
-        if use_t:
-            for r in range(TOP):
-                nc.sync.dma_start(out=grow[16 * r : 16 * r + 16, :], in_=gate[r, 0].rearrange("(c t) -> c t", t=P))
-        gates = {}
-        t0 = 0
-        for i, (m, w) in enumerate(OUT_CHUNKS):
-            if m != "T":
-                g = keep.tile([P, TOP, w], F32, name="g%d" % i)
-                nc.sync.dma_start(out=g[:], in_=gate.rearrange("r n t -> n r t")[:, :, t0 : t0 + w])
-                gates[i] = g
-            t0 = t0 + w
-
-        t0 = 0
-        for i, (w, ws) in enumerate(X_CHUNKS):
-            grouped = keep.tile([P, w, 4], BF16, name="grouped%d" % i, align_bytes=64)
-            for eng, a, z in (("s", 0, ws), ("v", ws, w)):
-                if z > a:
-                    dst = grouped[:, a:z, :].rearrange("p (c i) j -> p c j i", i=4)
-                    src = raws[i][:, :, a:z].rearrange("p j (c i) -> p c j i", i=4)
-                    if eng == "s":
-                        nc.scalar.copy(out=dst, in_=src)
-                    else:
-                        nc.vector.tensor_copy(out=dst, in_=src)
-            nc.vector.quantize_mx(
-                out=codes[:, t0 : t0 + w].bitcast(FP8X4),
-                scales=scales[:, t0 : t0 + w],
-                in_=grouped[:].rearrange("p w j -> p (w j)"),
+        for r in range(TOP):
+            nc.sync.dma_start(
+                out=gate_rows[SQUARES * r : SQUARES * (r + 1), :],
+                in_=gate[r, 0, :TURNED_GATE].rearrange("(c t) -> c t", t=P),
             )
-            t0 = t0 + w
+        gate_tiles = []
+        t0 = TURNED_GATE
+        for i, tokens in enumerate(PSUM_SUMS + [VECTOR_SUM]):
+            gate_tile = keep.tile([P, TOP, tokens], F32, name="gate_tile%d" % i)
+            nc.sync.dma_start(out=gate_tile[:], in_=gate.rearrange("r n t -> n r t")[:, :, t0 : t0 + tokens])
+            gate_tiles.append(gate_tile)
+            t0 = t0 + tokens
 
-        if use_t:
-            gps = psum.tile([P, 512], F32, name="gps", tag="back", bufs=2)
-            nc.tensor.transpose(gps[:, :P], grow[:], ident[:])
-            nc.scalar.copy(out=gcol[:], in_=gps[:, : TOP * 16])
+        t0 = 0
+        for i, (tokens, on_scalar) in enumerate(X_LOADS):
+            grouped = keep.tile([P, tokens, PACK], BF16, name="grouped%d" % i, align_bytes=64)
+            for copy, first, end in ((nc.scalar.copy, 0, on_scalar), (nc.vector.tensor_copy, on_scalar, tokens)):
+                copy(
+                    out=grouped[:, first:end, :].rearrange("p (c i) j -> p c j i", i=RUN),
+                    in_=x_tiles[i][:, :, first:end].rearrange("p j (c i) -> p c j i", i=RUN),
+                )
+            nc.vector.quantize_mx(
+                out=token_words[:, t0 : t0 + tokens].bitcast(FP8X4),
+                scales=token_scales[:, t0 : t0 + tokens],
+                in_=grouped[:].rearrange("p t j -> p (t j)"),
+            )
+            t0 = t0 + tokens
+
+        gate_turned = psum.tile([P, BANK], F32, name="gate_turned", tag="back", bufs=BACK_BANKS)
+        nc.tensor.transpose(gate_turned[:, :P], gate_rows[:], identity[:])
+        nc.scalar.copy(out=gate_cols[:], in_=gate_turned[:, : TOP * SQUARES])
 
         s0 = 0
-        for i, n in enumerate(SLOT_PIECES):
-            gw = keep.tile([P, n], U32, name="gw%d" % i, align_bytes=64)
-            gs = keep.tile([P, n], U8, name="gs%d" % i, align_bytes=64)
-            lst = offs_sb[:, s0 // 16 : (s0 + n) // 16]
-            nc.vector.tensor_copy(gw[:], codes[:].indirect(lst))
-            nc.vector.tensor_copy(gs[:], scales[:].indirect(lst))
-            for c0 in range(0, n, C):
+        for i, slots in enumerate(SLOT_PIECES):
+            slot_words = keep.tile([P, slots], U32, name="slot_words%d" % i, align_bytes=64)
+            slot_scales = keep.tile([P, slots], U8, name="slot_scales%d" % i, align_bytes=64)
+            nc.vector.tensor_copy(slot_words[:], token_words[:].indirect(entries(offs_sb, s0, slots)))
+            nc.vector.tensor_copy(slot_scales[:], token_scales[:].indirect(entries(offs_sb, s0, slots)))
+            for c0 in range(0, slots, C):
                 e = (s0 + c0) // C
-                acc = psum.tile([P, C], F32, name="acc", tag="acc", bufs=3)
+                product = psum.tile([P, C], F32, name="product", tag="product", bufs=PRODUCT_BANKS)
                 nc.tensor.matmul_mx(
-                    out=acc[:],
-                    lhsT=w_sb[:, e * 2 * N : (e + 1) * 2 * N].bitcast(FP4X4),
-                    lhsT_scale=ws_sb[:, e * N : (e + 1) * N],
-                    rhs=gw[:, c0 : c0 + C].bitcast(FP8X4),
-                    rhs_scale=gs[:, c0 : c0 + C],
+                    out=product[:],
+                    lhsT=weight_words[:, e * 2 * N : (e + 1) * 2 * N].bitcast(FP4X4),
+                    lhsT_scale=weight_scales[:, e * N : (e + 1) * N],
+                    rhs=slot_words[:, c0 : c0 + C].bitcast(FP8X4),
+                    rhs_scale=slot_scales[:, c0 : c0 + C],
                     start=True,
                     stop=True,
                 )
-                nc.scalar.activation(out=y[:, e * C : (e + 1) * C], in_=acc[:], func=IDENT, bias=b_sb[:, e : e + 1])
-            s0 = s0 + n
+                nc.scalar.activation(out=y[:, e * C : (e + 1) * C], in_=product[:], func=IDENTITY, bias=bias[:, e : e + 1])
+            s0 = s0 + slots
 
-        t0 = 0
-        for i, (m, w) in enumerate(OUT_CHUNKS):
-            if m == "T":
-                back = psum.tile([P, 512], F32, name="back", tag="back", bufs=2)
-                for r in range(TOP):
-                    part = keep.tile([P, w], F32, name="part%d_%d" % (i, r))
-                    nc.vector.tensor_copy(part[:], y[:].indirect(pos_sb[r][:, t0 // 16 : (t0 + w) // 16]))
-                    fwd = psum.tile([P, 512], F32, name="fwd", tag="fwd", bufs=3)
-                    for c in range(0, w, P):
-                        nc.tensor.transpose(fwd[:, c : c + P], part[:, c : c + P], ident[:])
-                    tt = keep.tile([P, w], F32, name="tt%d_%d" % (i, r))
-                    for c in range(0, w, P):
-                        col = 16 * r + (t0 + c) // P
-                        nc.scalar.activation(out=tt[:, c : c + P], in_=fwd[:, c : c + P], func=COPY, scale=gcol[:, col : col + 1])
-                    for c in range(0, w, P):
-                        nc.tensor.matmul(
-                            back[:, c : c + P], tt[:, c : c + P], ident[:],
-                            start=(r == 0 and c == 0), stop=(r == TOP - 1 and c == w - P), is_transpose=True,
-                        )
-                res = keep.tile([P, w], F32, name="res%d" % i)
-                nc.scalar.copy(out=res[:], in_=back[:, :w])
-                nc.scalar.dma_start(out=out[:, t0 : t0 + w], in_=res[:])
-                t0 = t0 + w
-                continue
-            parts = []
-            if m == "P":
-                fwd = psum.tile([P, 512], F32, name="fwd", tag="fwd", bufs=3)
+        def add_transposed(bank, values, tokens, r):
+            for c in range(0, tokens, P):
+                nc.tensor.matmul(
+                    bank[:, c : c + P],
+                    values[:, c : c + P],
+                    identity[:],
+                    start=(r == 0 and c == 0),
+                    stop=(r == TOP - 1 and c == tokens - P),
+                    is_transpose=True,
+                )
+
+        def gather_gated(i, t0, tokens, r):
+            gated = keep.tile([P, tokens], F32, name="gated%d_%d" % (i, r))
+            nc.vector.tensor_tensor(gated[:], y[:].indirect(entries(pos_sb[r], t0, tokens)), gate_tiles[i][:, r, :], MULT)
+            return gated
+
+        def store_bank(bank, t0, tokens):
+            result = keep.tile([P, tokens], F32, name="result%d" % t0)
+            nc.scalar.copy(out=result[:], in_=bank[:, :tokens])
+            nc.scalar.dma_start(out=out[:, t0 : t0 + tokens], in_=result[:])
+
+        summed = psum.tile([P, BANK], F32, name="summed", tag="back", bufs=BACK_BANKS)
+        for r in range(TOP):
+            picked = keep.tile([P, TURNED_GATE], F32, name="picked%d" % r)
+            nc.vector.tensor_copy(picked[:], y[:].indirect(entries(pos_sb[r], 0, TURNED_GATE)))
+            turned = psum.tile([P, BANK], F32, name="turned", tag="turn", bufs=TURN_BANKS)
+            for c in range(0, TURNED_GATE, P):
+                nc.tensor.transpose(turned[:, c : c + P], picked[:, c : c + P], identity[:])
+            scaled = keep.tile([P, TURNED_GATE], F32, name="scaled%d" % r)
+            for c in range(SQUARES):
+                col = SQUARES * r + c
+                nc.scalar.activation(
+                    out=scaled[:, c * P : (c + 1) * P], in_=turned[:, c * P : (c + 1) * P], func=COPY, scale=gate_cols[:, col : col + 1]
+                )
+            add_transposed(summed, scaled, TURNED_GATE, r)
+        store_bank(summed, 0, TURNED_GATE)
+
+        t0 = TURNED_GATE
+        for i, tokens in enumerate(PSUM_SUMS):
+            turned_sum = psum.tile([P, BANK], F32, name="turned_sum", tag="turn", bufs=TURN_BANKS)
             for r in range(TOP):
-                part = keep.tile([P, w], F32, name="part%d_%d" % (i, r))
-                picked = y[:].indirect(pos_sb[r][:, t0 // 16 : (t0 + w) // 16])
-                nc.vector.tensor_tensor(part[:], picked, gates[i][:, r, :], MULT)
-                parts.append(part)
-                if m == "P":
-                    for c in range(0, w, P):
-                        nc.tensor.matmul(
-                            fwd[:, c : c + P], part[:, c : c + P], ident[:],
-                            start=(r == 0 and c == 0), stop=(r == TOP - 1 and c == w - P), is_transpose=True,
-                        )
-            res = keep.tile([P, w], F32, name="res%d" % i)
-            if m == "V":
-                nc.vector.tensor_tensor(parts[0][:], parts[0][:], parts[1][:], ADD)
-                nc.vector.tensor_tensor(res[:], parts[0][:], parts[2][:], ADD)
-                nc.sync.dma_start(out=out[:, t0 : t0 + w], in_=res[:])
-            else:
-                tt = keep.tile([P, w], F32, name="tt%d" % i)
-                nc.scalar.copy(out=tt[:], in_=fwd[:, :w])
-                back = psum.tile([P, 512], F32, name="back", tag="back", bufs=2)
-                for c in range(0, w, P):
-                    nc.tensor.transpose(back[:, c : c + P], tt[:, c : c + P], ident[:])
-                nc.scalar.copy(out=res[:], in_=back[:, :w])
-                nc.scalar.dma_start(out=out[:, t0 : t0 + w], in_=res[:])
-            t0 = t0 + w
+                add_transposed(turned_sum, gather_gated(i, t0, tokens, r), tokens, r)
+            turned_sb = keep.tile([P, tokens], F32, name="turned_sb%d" % i)
+            nc.scalar.copy(out=turned_sb[:], in_=turned_sum[:, :tokens])
+            back = psum.tile([P, BANK], F32, name="back", tag="back", bufs=BACK_BANKS)
+            for c in range(0, tokens, P):
+                nc.tensor.transpose(back[:, c : c + P], turned_sb[:, c : c + P], identity[:])
+            store_bank(back, t0, tokens)
+            t0 = t0 + tokens
+
+        terms = [gather_gated(len(PSUM_SUMS), t0, VECTOR_SUM, r) for r in range(TOP)]
+        total = keep.tile([P, VECTOR_SUM], F32, name="total")
+        nc.vector.tensor_tensor(terms[0][:], terms[0][:], terms[1][:], ADD)
+        nc.vector.tensor_tensor(total[:], terms[0][:], terms[2][:], ADD)
+        nc.sync.dma_start(out=out[:, t0 : t0 + VECTOR_SUM], in_=total[:])

from contextlib import ExitStack

import concourse.mybir as mybir
from concourse.masks import make_identity

K, T, E, C, N = 512, 2048, 12, 256, 128
TOP = 3
PAD = 64
S = E * C
FLOPS = 2 * K * N * S

F32 = mybir.dt.float32
BF16 = mybir.dt.bfloat16
I32 = mybir.dt.int32
U32 = mybir.dt.uint32
U16 = mybir.dt.uint16
U8 = mybir.dt.uint8
FP8X4 = mybir.dt.float8_e4m3fn_x4
FP4X4 = mybir.dt.float4_e2m1fn_x4
MULT = mybir.AluOpType.mult
ADD = mybir.AluOpType.add
IDENTITY = mybir.ActivationFunctionType.Identity
COPY = mybir.ActivationFunctionType.Copy

P = 128
PACK = 4
STRIPE = 16
BANK = 512
RUN = 4

X_LOADS = [(512, 256), (512, 256), (512, 256), (256, 128), (128, 64), (128, 48)]

SLOT_PIECES = [1280, 1024, 512, 256]

TURNED_GATE = 512
PSUM_SUMS = [512, 512, 256]
VECTOR_SUM = 256
assert TURNED_GATE + sum(PSUM_SUMS) + VECTOR_SUM == T
SQUARES = TURNED_GATE // P

PRODUCT_BANKS, TURN_BANKS, BACK_BANKS = 3, 3, 2


def entries(list_tile, first, count):
    return list_tile[:, first // STRIPE : (first + count) // STRIPE]


def tile_moe_ecr_lin_bias_kernel(tc, xT, w_words, w_scales, b, gate, offs, pos1, pos2, pos3, out):
    nc = tc.nc
    with ExitStack() as ctx:
        keep = ctx.enter_context(tc.tile_pool(name="keep", bufs=1))
        psum = ctx.enter_context(tc.psum_pool(name="psum", bufs=1))

        offs_sb = keep.tile([P, S // STRIPE], U16, name="offs_sb")
        pos_sb = [keep.tile([P, T // STRIPE], U16, name="pos_sb%d" % r) for r in range(TOP)]
        token_words = keep.tile([P, T], U32, name="token_words", align_bytes=64)
        token_scales = keep.tile([P, T], U8, name="token_scales", align_bytes=64)
        weight_words = keep.tile([P, E * 2 * N], U8, name="weight_words", align_bytes=64)
        weight_scales = keep.tile([P, E * N], U8, name="weight_scales", align_bytes=64)
        bias = keep.tile([P, E], F32, name="bias")
        y = keep.tile([P, S + PAD], F32, name="y")
        identity = keep.tile([P, P], F32, name="identity")
        gate_rows = keep.tile([P, P], F32, name="gate_rows")
        gate_cols = keep.tile([P, TOP * SQUARES], F32, name="gate_cols")

        nc.gpsimd.memset(token_scales[:].bitcast(I32), 0)
        nc.gpsimd.memset(weight_scales[:].bitcast(I32), 0)
        nc.gpsimd.memset(y[:, S:], 0.0)
        nc.gpsimd.memset(gate_rows[:], 0.0)
        make_identity(nc, identity[:])

        x_rows = xT.rearrange("(p j) t -> p j t", j=PACK)
        x_tiles = []
        t0 = 0
        for i, (tokens, on_scalar) in enumerate(X_LOADS):
            x_tile = keep.tile([P, PACK, tokens], F32, name="x_tile%d" % i)
            nc.sync.dma_start(out=x_tile[:], in_=x_rows[:, :, t0 : t0 + tokens])
            x_tiles.append(x_tile)
            t0 = t0 + tokens
        nc.sync.dma_start(offs_sb[:], offs)
        nc.sync.dma_start(
            out=weight_words[:].bitcast(I32).rearrange("p (e c) -> p e c", e=E),
            in_=w_words.rearrange("e a p c -> p (e a) c").bitcast(I32),
        )
        for d in range(4):
            nc.sync.dma_start(
                out=weight_scales[d:P:32, :].bitcast(I32).rearrange("g (e c) -> g e c", e=E),
                in_=w_scales.rearrange("e a (g d) n -> d g (e a) n", d=4)[d].bitcast(I32),
            )
        nc.sync.dma_start(out=bias[:], in_=b)
        for r, pos in enumerate((pos1, pos2, pos3)):
            nc.sync.dma_start(pos_sb[r][:], pos)
        for r in range(TOP):
            nc.sync.dma_start(
                out=gate_rows[SQUARES * r : SQUARES * (r + 1), :],
                in_=gate[r, 0, :TURNED_GATE].rearrange("(c t) -> c t", t=P),
            )
        gate_tiles = []
        t0 = TURNED_GATE
        for i, tokens in enumerate(PSUM_SUMS + [VECTOR_SUM]):
            gate_tile = keep.tile([P, TOP, tokens], F32, name="gate_tile%d" % i)
            nc.sync.dma_start(out=gate_tile[:], in_=gate.rearrange("r n t -> n r t")[:, :, t0 : t0 + tokens])
            gate_tiles.append(gate_tile)
            t0 = t0 + tokens

        t0 = 0
        for i, (tokens, on_scalar) in enumerate(X_LOADS):
            grouped = keep.tile([P, tokens, PACK], BF16, name="grouped%d" % i, align_bytes=64)
            for copy, first, end in ((nc.scalar.copy, 0, on_scalar), (nc.vector.tensor_copy, on_scalar, tokens)):
                copy(
                    out=grouped[:, first:end, :].rearrange("p (c i) j -> p c j i", i=RUN),
                    in_=x_tiles[i][:, :, first:end].rearrange("p j (c i) -> p c j i", i=RUN),
                )
            nc.vector.quantize_mx(
                out=token_words[:, t0 : t0 + tokens].bitcast(FP8X4),
                scales=token_scales[:, t0 : t0 + tokens],
                in_=grouped[:].rearrange("p t j -> p (t j)"),
            )
            t0 = t0 + tokens

        gate_turned = psum.tile([P, BANK], F32, name="gate_turned", tag="back", bufs=BACK_BANKS)
        nc.tensor.transpose(gate_turned[:, :P], gate_rows[:], identity[:])
        nc.scalar.copy(out=gate_cols[:], in_=gate_turned[:, : TOP * SQUARES])

        s0 = 0
        for i, slots in enumerate(SLOT_PIECES):
            slot_words = keep.tile([P, slots], U32, name="slot_words%d" % i, align_bytes=64)
            slot_scales = keep.tile([P, slots], U8, name="slot_scales%d" % i, align_bytes=64)
            nc.vector.tensor_copy(slot_words[:], token_words[:].indirect(entries(offs_sb, s0, slots)))
            nc.vector.tensor_copy(slot_scales[:], token_scales[:].indirect(entries(offs_sb, s0, slots)))
            for c0 in range(0, slots, C):
                e = (s0 + c0) // C
                product = psum.tile([P, C], F32, name="product", tag="product", bufs=PRODUCT_BANKS)
                nc.tensor.matmul_mx(
                    out=product[:],
                    lhsT=weight_words[:, e * 2 * N : (e + 1) * 2 * N].bitcast(FP4X4),
                    lhsT_scale=weight_scales[:, e * N : (e + 1) * N],
                    rhs=slot_words[:, c0 : c0 + C].bitcast(FP8X4),
                    rhs_scale=slot_scales[:, c0 : c0 + C],
                    start=True,
                    stop=True,
                )
                nc.scalar.activation(out=y[:, e * C : (e + 1) * C], in_=product[:], func=IDENTITY, bias=bias[:, e : e + 1])
            s0 = s0 + slots

        def add_transposed(bank, values, tokens, r):
            for c in range(0, tokens, P):
                nc.tensor.matmul(
                    bank[:, c : c + P],
                    values[:, c : c + P],
                    identity[:],
                    start=(r == 0 and c == 0),
                    stop=(r == TOP - 1 and c == tokens - P),
                    is_transpose=True,
                )

        def gather_gated(i, t0, tokens, r):
            gated = keep.tile([P, tokens], F32, name="gated%d_%d" % (i, r))
            nc.vector.tensor_tensor(gated[:], y[:].indirect(entries(pos_sb[r], t0, tokens)), gate_tiles[i][:, r, :], MULT)
            return gated

        def store_bank(bank, t0, tokens):
            result = keep.tile([P, tokens], F32, name="result%d" % t0)
            nc.scalar.copy(out=result[:], in_=bank[:, :tokens])
            nc.scalar.dma_start(out=out[:, t0 : t0 + tokens], in_=result[:])

        summed = psum.tile([P, BANK], F32, name="summed", tag="back", bufs=BACK_BANKS)
        for r in range(TOP):
            picked = keep.tile([P, TURNED_GATE], F32, name="picked%d" % r)
            nc.vector.tensor_copy(picked[:], y[:].indirect(entries(pos_sb[r], 0, TURNED_GATE)))
            turned = psum.tile([P, BANK], F32, name="turned", tag="turn", bufs=TURN_BANKS)
            for c in range(0, TURNED_GATE, P):
                nc.tensor.transpose(turned[:, c : c + P], picked[:, c : c + P], identity[:])
            scaled = keep.tile([P, TURNED_GATE], F32, name="scaled%d" % r)
            for c in range(SQUARES):
                col = SQUARES * r + c
                nc.scalar.activation(
                    out=scaled[:, c * P : (c + 1) * P], in_=turned[:, c * P : (c + 1) * P], func=COPY, scale=gate_cols[:, col : col + 1]
                )
            add_transposed(summed, scaled, TURNED_GATE, r)
        store_bank(summed, 0, TURNED_GATE)

        t0 = TURNED_GATE
        for i, tokens in enumerate(PSUM_SUMS):
            turned_sum = psum.tile([P, BANK], F32, name="turned_sum", tag="turn", bufs=TURN_BANKS)
            for r in range(TOP):
                add_transposed(turned_sum, gather_gated(i, t0, tokens, r), tokens, r)
            turned_sb = keep.tile([P, tokens], F32, name="turned_sb%d" % i)
            nc.scalar.copy(out=turned_sb[:], in_=turned_sum[:, :tokens])
            back = psum.tile([P, BANK], F32, name="back", tag="back", bufs=BACK_BANKS)
            for c in range(0, tokens, P):
                nc.tensor.transpose(back[:, c : c + P], turned_sb[:, c : c + P], identity[:])
            store_bank(back, t0, tokens)
            t0 = t0 + tokens

        terms = [gather_gated(len(PSUM_SUMS), t0, VECTOR_SUM, r) for r in range(TOP)]
        total = keep.tile([P, VECTOR_SUM], F32, name="total")
        nc.vector.tensor_tensor(terms[0][:], terms[0][:], terms[1][:], ADD)
        nc.vector.tensor_tensor(total[:], terms[0][:], terms[2][:], ADD)
        nc.sync.dma_start(out=out[:, t0 : t0 + VECTOR_SUM], in_=total[:])
